import numpy as np, ml_dtypes
CORES = [5,21,45,77,85,101,109,125,133,141,189,213]
N = 12
GR, GC = 2, 6
L, KA, KB, F = 6, 1, 3, 32
def setup_inputs(rng):
    return {"a": rng.standard_normal((N, 128, KA * 128), dtype=np.float32).astype(ml_dtypes.bfloat16), "b": rng.standard_normal((N, 128, KB * F), dtype=np.float32).astype(ml_dtypes.bfloat16)}
def reference(a, b):
    A, B = a.astype(np.float64), b.astype(np.float64)
    y = np.zeros((N, 128, F))
    for i in range(GR):
        for j in range(GC):
            for k in range(L):
                At = A[i * GC + k // KA][:, 128 * (k % KA):128 * (k % KA) + 128]
                Bt = B[(k // KB) * GC + j][:, F * (k % KB):F * (k % KB) + F]
                y[i * GC + j] += At.T @ Bt
    return {"y": y.astype(ml_dtypes.bfloat16 if a.dtype != np.float64 else np.float64)}

from concourse.bass import DstId, RemoteDMATransfer

GR, GC, KB, F, P = 2, 6, 3, 32, 128

FEED_A, FEED_B = 4, 2

SCRATCH = {
    "astage": ("dram", [P, P], "bfloat16"),
    "bstage": ("dram", [P, KB * F], "bfloat16"),
    "aland": ("sbuf", [P, GC * P], "bfloat16"),
    "bown": ("sbuf", [P, KB * F], "bfloat16"),
    "bland": ("sbuf", [P, KB * F], "bfloat16"),
    "ysb": ("sbuf", [P, F], "bfloat16"),
    "acc": ("psum", [P, F], "float32"),
}
SEMAPHORES = ["astaged", "bstaged", "own", "fed", "sent", "gotb", "summed", "rounded", "stored"] + [
    "gota%d" % k for k in range(GC)]


def _bits(mask):
    return [e for e in range(mask.bit_length()) if (mask >> e) & 1]


def _mask(sel):
    return sum(1 << e for e in sel)


def _common(topo, src, dsts):
    m = topo.mask(src, dsts[0])
    for d in dsts[1:]:
        m &= topo.mask(src, d)
    return m


def _chip_cores(topo, c):
    n = topo.CORES_PER_CHIP
    return [x for x in range(max(0, c - n + 1), c + n) if topo.host(x) == topo.host(c) and topo.chip(x) == topo.chip(c)]


def _plan(cores, topo):
    senders, relay, arrive, inload = [], {}, {}, {}
    for s, cs in enumerate(cores):
        row, col = divmod(s, GC)
        peers = [row * GC + j for j in range(GC) if j != col]
        partner = (GR - 1 - row) * GC + col
        direct = [d for d in peers if topo.may_write(cs, cores[d])]
        cross = [d for d in peers if d not in direct]
        b_direct = topo.may_write(cs, cores[partner]) and len(direct) < len(cross)
        tasks = ([] if b_direct else [("b", partner)]) + [("a", d) for d in cross]
        owners = [h for h in _chip_cores(topo, cs) if h != cs and all(topo.may_write(h, cores[d]) for _, d in tasks)]
        jobs, outload = {h: [] for h in owners}, {}
        for kind, d in tasks:
            fit = [h for h in owners if all(kk == kind for kk, _ in jobs[h])]
            h = min(fit, key=lambda h: (len(jobs[h]), inload.get((d, topo.die(h)), 0), outload.get(topo.die(h), 0),
                                        topo.die(h) != topo.die(cs), h))
            jobs[h].append((kind, d))
            inload[(d, topo.die(h))] = inload.get((d, topo.die(h)), 0) + 1
            outload[topo.die(h)] = outload.get(topo.die(h), 0) + 1
        jl = sorted([(h, j[0][0], [d for _, d in j]) for h, j in jobs.items() if j], key=lambda x: (-len(x[2]), x[0]))
        a_first = b_direct or any(len(ds) > 1 for _, _, ds in jl)
        for h, kind, ds in jl:
            relay[h] = (s, kind, ds)
            n = len(_bits(_common(topo, h, [cores[d] for d in ds])))
            for d in ds:
                arrive[(kind, s, d)] = ((1 + len(ds) if kind == "a" else 2.5) if a_first else (2.5 if kind == "a" else 2), n)
        n = len(_bits(_common(topo, cs, [cores[d] for d in direct] + ([cores[partner]] if b_direct else []))))
        for d in direct:
            arrive[("a", s, d)] = (1, n)
        if b_direct:
            arrive[("b", s, partner)] = (1.5, n)
        senders.append((direct, b_direct, a_first, jl))
    return senders, relay, arrive


def _send(g, T, topo, src_core, dst_cores, mask, sem, src, dst):
    ids = []
    for d in dst_cores:
        rid, pid = topo.addr(d, src_core)
        ids.append(DstId(rid=rid, pnc=pid))
    g.remote_dma_fused([RemoteDMATransfer(dst_ids=ids, dma_engine_mask=mask, remote_sem=sem, srcs=[src],
                                          dsts=[dst] * len(ids))], local_sem=T.sem.sent)
    return len(_bits(mask))


def rank_program(g, core, T, topo):
    cores = list(T.cores)
    senders, relay, arrive = _plan(cores, topo)
    rank = T.rank_of(core)

    if rank is None:
        if core not in relay:
            return
        s, kind, ds = relay[core]
        dst_cores = [cores[d] for d in ds]
        m = _common(topo, core, dst_cores)
        k = s % GC
        if kind == "a":
            g.wait_ge(T.sem.fed, FEED_A)
            n = _send(g, T, topo, core, dst_cores, m, T.sem["gota%d" % k], T.astage[:, :], T.aland[:, P * k:P * k + P])
        else:
            g.wait_ge(T.sem.fed, FEED_B)
            n = _send(g, T, topo, core, dst_cores, m, T.sem.gotb, T.bstage[:, :], T.bland[:, :])
        g.wait_ge(T.sem.sent, n)
        return

    row, col = divmod(rank, GC)
    partner = (GR - 1 - row) * GC + col
    direct, b_direct, a_first, jobs = senders[rank]
    slot = T.aland[:, P * col:P * col + P]

    g.sync.dma_start(T.astage[:, :], T.a[:, :]).then_inc(T.sem.astaged, 16)
    g.scalar.dma_start(T.bstage[:, :], T.b[:, :]).then_inc(T.sem.bstaged, 16)
    g.sync.dma_start(slot, T.a[:, :]).then_inc(T.sem.own, 16)
    g.scalar.dma_start(T.bown[:, :], T.b[:, :]).then_inc(T.sem.own, 16)

    off = _common(topo, core, [cores[d] for d in direct] + ([cores[partner]] if b_direct else []))
    a_relays = [h for h, kind, _ in jobs if kind == "a"]
    b_relays = [h for h, kind, _ in jobs if kind == "b"]
    spare = _bits(_common(topo, core, a_relays + b_relays) & ~off)
    sent = 0
    for kind in ("ab" if a_first else "ba"):
        if kind == "a":
            g.wait_ge(T.sem.astaged, 16)
            sent += _send(g, T, topo, core, a_relays, _mask(spare[0::2][:FEED_A]), T.sem.fed, T.astage[:, :], T.astage[:, :])
        else:
            g.wait_ge(T.sem.bstaged, 16)
            if b_relays:
                sent += _send(g, T, topo, core, b_relays, _mask(spare[1::2][:FEED_B]), T.sem.fed, T.bstage[:, :],
                              T.bstage[:, :])

    sent += _send(g, T, topo, core, [cores[d] for d in direct], off, T.sem["gota%d" % col], T.astage[:, :], slot)
    if b_direct:
        sent += _send(g, T, topo, core, [cores[partner]], off, T.sem.gotb, T.bstage[:, :], T.bland[:, :])

    terms = []
    for k in range(GC):
        ca = 0 if k == col else arrive[("a", row * GC + k, rank)][0]
        cb = 0 if k // KB == row else arrive[("b", partner, rank)][0]
        terms.append((max(ca, cb), ca, k))
    terms.sort()
    g.tensor.wait_ge(T.sem.own, 32)
    have_b = False
    mm = None
    for n, (_, _, k) in enumerate(terms):
        if k != col:
            g.tensor.wait_ge(T.sem["gota%d" % k], arrive[("a", row * GC + k, rank)][1])
        if k // KB != row and not have_b:
            g.tensor.wait_ge(T.sem.gotb, arrive[("b", partner, rank)][1])
            have_b = True
        t = k % KB
        rhs = T.bown[:, F * t:F * t + F] if k // KB == row else T.bland[:, F * t:F * t + F]
        mm = g.tensor.matmul(T.acc[:, :], T.aland[:, P * k:P * k + P], rhs, start=(n == 0), stop=(n == GC - 1))
    mm.then_inc(T.sem.summed, 1)
    g.vector.wait_ge(T.sem.summed, 1)
    g.vector.tensor_copy(T.ysb[:, :], T.acc[:, :]).then_inc(T.sem.rounded, 1)
    g.sync.wait_ge(T.sem.rounded, 1)
    g.sync.dma_start(T.y[:, :], T.ysb[:, :]).then_inc(T.sem.stored, 16)
    g.sync.wait_ge(T.sem.stored, 16)
    g.wait_ge(T.sem.sent, sent)
